import numpy as np, ml_dtypes
CORES = [76,84,92,100,108,116,124]
N = 7
TK = 64
COEF = [[3,-2,-2,2,3,2,3],[3,1,3,3,-1,2,3],[1,2,2,-1,-1,-1,3],[-2,1,-2,3,3,-2,2],[-1,-2,3,-1,1,-2,1],[2,2,1,-1,2,-1,-2],[3,-2,2,3,2,-1,2]]
def setup_inputs(rng):
    return {"x": rng.standard_normal((N, 128, TK), dtype=np.float32).astype(ml_dtypes.bfloat16), "a": (rng.standard_normal((N, 128, 128), dtype=np.float32) / 11).astype(ml_dtypes.bfloat16)}
def setup_inputs_big(rng):
    d = setup_inputs(rng)
    for k in ("x", "a"): d[k] = (d[k].astype(np.float32) * 1024.0).astype(d[k].dtype)
    return d
def setup_inputs_small(rng):
    d = setup_inputs(rng)
    for k in ("x", "a"): d[k] = (d[k].astype(np.float32) * (1 / 1024.0)).astype(d[k].dtype)
    return d
def setup_inputs_apart(rng):
    d = setup_inputs(rng)
    f = (10.0 ** rng.permutation(np.linspace(-1.5, 1.5, N))).astype(np.float32).reshape(N, 1, 1)
    for k in ("x", "a"): d[k] = (d[k].astype(np.float32) * f).astype(d[k].dtype)
    return d
def reference(x, a):
    X, A = x.astype(np.float64), a.astype(np.float64)
    y = np.stack([A[r].T @ sum(COEF[r][j] * X[j] for j in range(N)) for r in range(N)])
    return {"y": y.astype(ml_dtypes.bfloat16)}

from concourse.bass import DstId, RemoteDMATransfer
from concourse.mybir import AluOpType

NR = 7
W = 64
NDIRECT = 2
FEED_ENG = 2
SEND_ENG = 8
DIRECT_ENG = 8

SCRATCH = {
    "xd": ("dram", [128, W], "bfloat16"),
    "xr": ("dram", [128, W], "bfloat16"),
    "xg": ("sbuf", [128, NR * W], "bfloat16"),
    "a1": ("sbuf", [128, 128], "bfloat16"),
    "kc": ("sbuf", [128, 4 * 128], "bfloat16"),
    "ac": ("sbuf", [128, 4 * 128], "bfloat16"),
    "acc": ("psum", [128, W], "float32"),
    "ys": ("sbuf", [128, W], "bfloat16"),
}
SEMAPHORES = ["lx", "la", "lo", "ms", "sc", "fed", "early", "late", "sent", "mm", "cp", "st"]


def bits(m):
    return [i for i in range(m.bit_length()) if (m >> i) & 1]


def to_mask(engines):
    return sum(1 << e for e in engines)


def route(topo, s, d):
    cs, cd, di = topo.chip(s), topo.chip(d), topo.die(s)
    if cs == cd:
        return []
    if topo.same_plane(cs, cd):
        return [("out", cs, di), ("in", cd, di)]
    hops = [("mate", cs, di)]
    if not topo.mates(cs, cd):
        m = [c for c in range(topo.CHIPS) if topo.mates(cs, c)][0]
        hops += [("out", m, di), ("in", cd, di)]
    return hops


def make_plan(cores, topo):
    n = len(cores)
    every = range(topo.CORES_PER_CHIP * topo.CHIPS)
    direct, todo = [], []
    for j in range(n):
        others = [(j + k) % n for k in range(1, n)]
        own = [r for r in others if topo.may_write(cores[j], cores[r])]
        if len(own) > NDIRECT:
            own = own[:(NDIRECT + 1) // 2] + own[len(own) - NDIRECT // 2:]
        direct += [(j, r) for r in own]
        todo += [(j, r) for r in others if r not in own]
    todo.sort(key=lambda p: -len(route(topo, cores[p[0]], cores[p[1]])))
    used, load, relay = set(cores), {}, []
    for j, r in todo:
        free = [c for c in every if topo.chip(c) == topo.chip(cores[j]) and c not in used
                and topo.may_write(c, cores[r])]

        def cost(c):
            on = [load.get(l, 0) for l in route(topo, c, cores[r])]
            return (max(on), sum(on), topo.die(c) == topo.die(cores[j]))

        h = min(free, key=cost)
        used.add(h)
        for l in route(topo, h, cores[r]):
            load[l] = load.get(l, 0) + 1
        relay.append((j, r, h))
    return direct, relay


def dst_id(topo, c):
    rid, pid, _se = topo.addr(c)
    return DstId(rid=rid, pnc=pid)


def rank_program(g, core, T, topo):
    cores = list(T.cores)
    direct, relay = make_plan(cores, topo)
    S = T.sem
    rank = T.rank_of(core)

    if rank is None:
        mine = [(j, r) for (j, r, h) in relay if h == core]
        if not mine:
            return
        j, r = mine[0]
        rid, pid, _se = topo.addr(cores[r])
        g.wait_ge(S.fed, FEED_ENG)
        g.remote_dma(T.xg[:, j * W:(j + 1) * W], T.xr[:], S.late, S.sent, pid, rid,
                     to_mask(bits(topo.mask(core, cores[r]))[:SEND_ENG]))
        g.wait_ge(S.sent, SEND_ENG)
        return

    coef = T.tables["COEF"][rank]
    slot = lambda j: T.xg[:, j * W:(j + 1) * W]

    g.sync.dma_start(T.xd[:], T.x[:]).then_inc(S.lx, 16)
    g.sync.dma_start(T.a1[:], T.a[:]).then_inc(S.la, 16)
    g.sync.dma_start(slot(rank), T.x[:]).then_inc(S.lo, 16)

    helpers = [h for (j, r, h) in relay if j == rank]
    mydirect = [r for (j, r) in direct if j == rank]
    away = to_mask(bits(topo.mask(core, cores[mydirect[0]]))[:DIRECT_ENG])
    chip_only = [e for e in bits(topo.mask(core, helpers[0])) if not (away >> e) & 1]
    g.wait_ge(S.lx, 16)
    g.remote_dma_fused(
        [RemoteDMATransfer(dst_ids=[dst_id(topo, h)], dma_engine_mask=to_mask(chip_only[i * FEED_ENG:(i + 1) * FEED_ENG]),
                           remote_sem=S.fed, src=T.xd[:], dst=T.xr[:]) for i, h in enumerate(helpers)],
        local_sem=S.sent)
    g.remote_dma_fused(
        [RemoteDMATransfer(dst_ids=[dst_id(topo, cores[r]) for r in mydirect], dma_engine_mask=away,
                           remote_sem=S.early, srcs=[T.xd[:]], dsts=[slot(rank) for r in mydirect])],
        local_sem=S.sent)

    v = g.vector
    cs = sorted(set(c for c in coef if c != 1))
    blk = {c: slice(i * 128, (i + 1) * 128) for i, c in enumerate(cs)}
    for c in cs:
        v.memset(T.kc[:, blk[c]], float(c)).then_inc(S.ms, 1)
    v.wait_ge(S.ms, len(cs))
    v.wait_ge(S.la, 16)
    for c in cs:
        v.tensor_tensor(T.ac[:, blk[c]], T.a1[:], T.kc[:, blk[c]], AluOpType.mult).then_inc(S.sc, 1)

    te = g.tensor
    first = [j for (j, r) in direct if r == rank]
    last = [j for (j, r, h) in relay if r == rank]
    order = [rank] + first + last

    def mm(j):
        lhs = T.a1[:] if coef[j] == 1 else T.ac[:, blk[coef[j]]]
        return te.matmul(T.acc[:], lhs, slot(j), start=(j == order[0]), stop=(j == order[-1]))

    te.wait_ge(S.la, 16)
    te.wait_ge(S.sc, len(cs))
    te.wait_ge(S.lo, 16)
    mm(rank)
    te.wait_ge(S.early, DIRECT_ENG * len(first))
    for j in first:
        mm(j)
    te.wait_ge(S.late, SEND_ENG * len(last))
    for j in last[:-1]:
        mm(j)
    mm(last[-1]).then_inc(S.mm, 1)

    v.wait_ge(S.mm, 1)
    v.tensor_copy(T.ys[:], T.acc[:]).then_inc(S.cp, 1)
    g.scalar.wait_ge(S.cp, 1)
    g.scalar.dma_start(T.y[:], T.ys[:]).then_inc(S.st, 16)
    g.scalar.wait_ge(S.st, 16)
    g.wait_ge(S.sent, FEED_ENG * len(helpers) + DIRECT_ENG)
